import numpy as np
import ml_dtypes


def mxq(x, axis, fmt="e4m3"):
    dtype, down = {"e4m3": (ml_dtypes.float8_e4m3fn, 7), "e5m2": (ml_dtypes.float8_e5m2, 14)}[fmt]
    v = np.moveaxis(np.asarray(x, np.float32).astype(ml_dtypes.bfloat16).astype(np.float64), axis, -1)
    blocks = v.reshape(v.shape[:-1] + (-1, 32))
    amax = np.abs(blocks).max(-1, keepdims=True)
    byte = np.maximum(np.where(amax > 0, np.frexp(amax)[1] - 1 + 127, 0) - down, 1)
    scale = np.exp2(byte - 127.0)
    codes = (blocks / scale).astype(np.float32).astype(dtype).astype(np.float64)
    return np.moveaxis((codes * scale).reshape(v.shape), -1, axis)


WIDE = False


def mx_kscale(k):
    if not WIDE:
        return np.ones(k)
    levels = np.array([10, -10, 5, -5, 0])
    if k % 512:
        return np.exp2(np.random.permutation(np.resize(levels, k // 32))).repeat(32)
    a = np.empty((k // 512, 16))
    for p in range(k // 512):
        a[p, :8] = np.random.permutation(np.resize(levels, 8))
        for g in range(8):
            far = levels[np.abs(levels - a[p, g]) >= 10]
            a[p, g + 8] = far[np.random.randint(len(far))]
    return np.exp2(a.ravel()).repeat(32)


def f64(x):
    return np.asarray(x).astype(np.float64)


def striped(idx):
    return np.tile(idx.reshape(-1, 16).T, (8, 1)).astype(np.uint16)


def unstriped(offs):
    return offs[:16].T.reshape(-1).astype(np.int64)


def pack_weight(w):
    k, n = w.shape
    w = f64(np.asarray(w, np.float32).astype(ml_dtypes.bfloat16)).reshape(k // 32, 32, n)
    amax = np.abs(w).max(1)
    byte = np.clip(np.where(amax > 0, np.frexp(amax)[1] - 1 + 127 - 7, 1), 1, 254)
    scaled = (w * np.exp2(127.0 - byte)[:, None, :]).reshape(k, n).astype(np.float32)
    words = np.ascontiguousarray(scaled.reshape(k // 512, 128, 4, n).transpose(0, 1, 3, 2)).astype(ml_dtypes.float8_e4m3fn).view(np.uint8)
    return words, np.ascontiguousarray(byte.astype(np.uint8).reshape(k // 512, 16, n))


def unpack_weight(words, scales):
    g, p, n, _ = words.shape
    vals = np.ascontiguousarray(words).view(ml_dtypes.float8_e4m3fn).astype(np.float64) * np.repeat(np.exp2(scales.astype(np.float64) - 127.0), 8, axis=1)[..., None]
    return vals.transpose(0, 1, 3, 2).reshape(g * 512, n)


def planes(y):
    n, m = y.shape
    v = y.astype(np.float32).astype(ml_dtypes.bfloat16).astype(np.float64).reshape(n // 32, 32, m)
    top = np.abs(v).max(1)
    byte = np.clip(np.where(top > 0, np.frexp(top)[1] - 1 + 127 - 7, 1), 1, 254)
    codes = (v * np.exp2(127.0 - byte)[:, None, :]).reshape(n, m).astype(np.float32).astype(ml_dtypes.float8_e4m3fn).view(np.uint8)
    words = codes.reshape(n // 512, 128, 4, m).transpose(0, 1, 3, 2)
    return np.ascontiguousarray(words), np.ascontiguousarray(byte.astype(np.uint8).reshape(n // 512, 16, m))


K, T, S, N, W, G = 512, 1024, 512, 512, 1024, 2048
P = 2 ** 7


def setup_inputs():
    n = np.random.standard_normal
    s = mx_kscale(K)[:, None]
    packed_xT = pack_weight(n((K, T)) * s)
    packed_eT = pack_weight(n((K, W)) * s)
    packed_dT = pack_weight(n((K, G)) * s)
    return {
        "x_words": packed_xT[0],
        "x_scales": packed_xT[1],
        "e_words": packed_eT[0],
        "e_scales": packed_eT[1],
        "d_words": packed_dT[0],
        "d_scales": packed_dT[1],
        "att0": (np.tile(n(T) * 0.7, (P, 1))).astype(np.float32),
        "att1": (np.tile(n(T) * 0.7, (P, 1))).astype(np.float32),
        "att2": (np.tile(n(T) * 0.7, (P, 1))).astype(np.float32),
        "w1": (n((K, N)) / np.sqrt(K) / s).astype(np.float32),
        "w2": (n((K, N)) / np.sqrt(K) / s).astype(np.float32),
        "w3": (n((K, N)) / np.sqrt(K) / s).astype(np.float32),
        "offs": striped(np.random.permutation(T)[:S]),
        "shop": striped(np.random.permutation(W)[:S]),
        "brand": striped(np.random.permutation(G)[:S]),
    }


def reference(x_words, x_scales, e_words, e_scales, d_words, d_scales, att0, att1, att2, w1, w2, w3, offs, shop, brand):
    xq = unpack_weight(x_words, x_scales)[:, unstriped(offs)]
    y0 = mxq(f64(w1), 0, "e4m3").T @ xq
    a0 = np.exp(f64(att0)[:1][:, unstriped(offs)])
    e_shop = unpack_weight(e_words, e_scales)[:, unstriped(shop)]
    y1 = mxq(f64(w2), 0, "e4m3").T @ e_shop
    a1 = np.exp(f64(att1)[:1][:, unstriped(offs)])
    d_brand = unpack_weight(d_words, d_scales)[:, unstriped(brand)]
    y2 = mxq(f64(w3), 0, "e4m3").T @ d_brand
    a2 = np.exp(f64(att2)[:1][:, unstriped(offs)])
    num = y0 * a0 + y1 * a1 + y2 * a2
    den = a0 + a1 + a2
    out_0 = num / den
    return (out_0,) + planes(out_0)

@@ -1,0 +1,214 @@
+from contextlib import ExitStack
+
+import concourse.mybir as mybir
+from concourse.masks import make_identity
+
+F32 = mybir.dt.float32
+BF16 = mybir.dt.bfloat16
+I32 = mybir.dt.int32
+U32 = mybir.dt.uint32
+U16 = mybir.dt.uint16
+U8 = mybir.dt.uint8
+FP8X4 = mybir.dt.float8_e4m3fn_x4
+ALU = mybir.AluOpType
+ACT = mybir.ActivationFunctionType
+AX = mybir.AxisListType
+
+P = 128
+PACK = 4
+S = 512
+N = 512
+K = 512
+BLOCKS = S // P
+FLOPS = 3 * 2 * K * N * S
+
+
+def tile_picked_yeges_avg_po_kernel(
+    tc, x_words, x_scales, e_words, e_scales, d_words, d_scales, att0, att1, att2, w1, w2, w3, offs, shop, brand, out_0, out_1, out_2
+):
+    nc = tc.nc
+    words_in = [x_words, e_words, d_words]
+    scales_in = [x_scales, e_scales, d_scales]
+    lists_in = [offs, shop, brand]
+    atts = [att0, att1, att2]
+    ws = [w1, w2, w3]
+    widths = [w.shape[2] for w in words_in]
+
+    with ExitStack() as ctx:
+        keep = ctx.enter_context(tc.tile_pool(name="keep", bufs=1))
+        stage = ctx.enter_context(tc.tile_pool(name="stage", bufs=4))
+        ps_out = ctx.enter_context(tc.psum_pool(name="ps_out", bufs=1))
+        ps_y = ctx.enter_context(tc.psum_pool(name="ps_y", bufs=4))
+
+        lists = [keep.tile([P, S // 16], U16, name=f"list{i}") for i in range(3)]
+        word_tab = [keep.tile([P, widths[i]], U32, name=f"word_tab{i}", align_bytes=64) for i in range(3)]
+        scale_tab = [keep.tile([P, widths[i]], U8, name=f"scale_tab{i}", align_bytes=64) for i in range(3)]
+        att_tab = keep.tile([P, widths[0]], F32, name="att_tab", align_bytes=64)
+        w_raw = [keep.tile([P, PACK, N], F32, name=f"w_raw{i}", align_bytes=64) for i in range(3)]
+        ident = keep.tile([P, P], F32, name="ident", align_bytes=64)
+
+        nc.vector.memset(scale_tab[0][:].bitcast(I32), 0)
+        nc.vector.memset(scale_tab[1][:].bitcast(I32), 0)
+        nc.vector.memset(att_tab[:], 0.0)
+        nc.vector.memset(scale_tab[2][:].bitcast(I32), 0)
+        make_identity(nc, ident[:])
+
+        def load_scales(eng, i):
+            for q in range(4):
+                eng.dma_start(
+                    out=scale_tab[i][32 * q : 32 * q + 4, :].bitcast(I32),
+                    in_=scales_in[i][0, 4 * q : 4 * q + 4, :].bitcast(I32),
+                )
+
+        def load_words(i):
+            nc.sync.dma_start(
+                out=word_tab[i][:].bitcast(I32),
+                in_=words_in[i][0].rearrange("p c r -> p (c r)").bitcast(I32),
+            )
+
+        def load_weight(i):
+            nc.sync.dma_start(out=w_raw[i][:], in_=ws[i].rearrange("(p r) n -> p r n", r=PACK))
+
+        for i in range(3):
+            nc.sync.dma_start(lists[i][:], lists_in[i])
+        load_scales(nc.sync, 0)
+        load_weight(0)
+        load_scales(nc.sync, 1)
+        load_words(0)
+        load_weight(1)
+        load_words(1)
+        load_weight(2)
+        load_words(2)
+        for i in range(3):
+            nc.gpsimd.dma_start(out=att_tab[i : i + 1, :], in_=atts[i][0:1, :])
+        load_scales(nc.gpsimd, 2)
+
+        g_words = [keep.tile([P, S], U32, name=f"g_words{i}", align_bytes=64) for i in range(3)]
+        g_scales = [keep.tile([P, S], U8, name=f"g_scales{i}", align_bytes=64) for i in range(3)]
+        w_bf = [keep.tile([P, N, PACK], BF16, name=f"w_bf{i}", align_bytes=64) for i in range(3)]
+        w_codes = [keep.tile([P, N], U32, name=f"w_codes{i}", align_bytes=64) for i in range(3)]
+        w_scales = [keep.tile([P, N], U8, name=f"w_scales{i}", align_bytes=64) for i in range(3)]
+        out_banks = [ps_out.tile([P, PACK, P], F32, name=f"out_bank{b}") for b in range(BLOCKS)]
+
+        def gather_scales(i):
+            nc.vector.tensor_copy(g_scales[i][:], scale_tab[i][:].indirect(lists[i][:]))
+
+        def gather_words(i, pieces):
+            n = S // pieces
+            for h in range(pieces):
+                nc.vector.tensor_copy(
+                    g_words[i][:, h * n : (h + 1) * n],
+                    word_tab[i][:].indirect(lists[i][:, h * n // 16 : (h + 1) * n // 16]),
+                )
+
+        def interleave(eng, dst, src):
+            d = dst.rearrange("p (c i) r -> p c r i", i=4)
+            s = src.rearrange("p r (c i) -> p c r i", i=4)
+            if eng is nc.scalar:
+                nc.scalar.copy(d, s)
+            else:
+                nc.vector.tensor_copy(d, s)
+
+        def quantize_weight(i):
+            nc.vector.quantize_mx(
+                out=w_codes[i][:].bitcast(FP8X4),
+                scales=w_scales[i][:],
+                in_=w_bf[i][:].rearrange("p n r -> p (n r)"),
+            )
+
+        def product(i, b, on_scalar):
+            cols = slice(b * P, (b + 1) * P)
+            y = ps_y.tile([P, N], F32, name="y")
+            nc.tensor.matmul_mx(
+                out=y[:],
+                lhsT=g_words[i][:, cols].bitcast(FP8X4),
+                lhsT_scale=g_scales[i][:, cols],
+                rhs=w_codes[i][:].bitcast(FP8X4),
+                rhs_scale=w_scales[i][:],
+                start=True,
+                stop=True,
+            )
+            u = stage.tile([P, PACK, P], F32, name="u", align_bytes=64)
+            dealt = y[:].rearrange("j (p t) -> j t p", t=PACK)
+            if on_scalar:
+                nc.scalar.activation(u[:], dealt, ACT.Copy, scale=share[:, b, i : i + 1])
+            else:
+                nc.vector.tensor_scalar(u[:], dealt, share[:, b, i : i + 1], None, ALU.mult)
+            return u
+
+        def turn(i, b, u):
+            for t in range(PACK):
+                nc.tensor.matmul(
+                    out_banks[b][:, t, :],
+                    lhsT=u[:, t, :],
+                    rhs=ident[:],
+                    is_transpose=True,
+                    start=(i == 0 and t == 0),
+                    stop=(i == 2 and t == PACK - 1),
+                )
+
+        gather_scales(0)
+        interleave(nc.scalar, w_bf[0][:], w_raw[0][:])
+        gather_scales(1)
+
+        g_att = keep.tile([P, S], F32, name="g_att", align_bytes=64)
+        nc.vector.tensor_copy(g_att[:], att_tab[:].indirect(lists[0][:]))
+        att_t = ps_y.tile([P, BLOCKS, P], F32, name="y")
+        for b in range(BLOCKS):
+            nc.tensor.transpose(att_t[:, b, :], g_att[:, b * P : (b + 1) * P], ident[:])
+        top = keep.tile([P, BLOCKS], F32, name="top")
+        shifted = keep.tile([P, BLOCKS, 3], F32, name="shifted")
+        expd = keep.tile([P, BLOCKS, 3], F32, name="w_raw0", align_bytes=64)
+        den = keep.tile([P, BLOCKS], F32, name="den")
+        rden = keep.tile([P, BLOCKS], F32, name="rden")
+        share = keep.tile([P, BLOCKS, 3], F32, name="share")
+        gather_words(0, 1)
+        nc.vector.tensor_reduce(top[:], att_t[:, :, 0:3], AX.X, ALU.max)
+        nc.vector.tensor_tensor(shifted[:], att_t[:, :, 0:3], top[:].unsqueeze(2).to_broadcast([P, BLOCKS, 3]), ALU.subtract)
+        nc.scalar.activation(expd[:], shifted[:], ACT.Exp)
+        quantize_weight(0)
+        nc.vector.tensor_reduce(den[:], expd[:], AX.X, ALU.add)
+        nc.vector.reciprocal(rden[:], den[:])
+        nc.vector.tensor_tensor(share[:], expd[:], rden[:].unsqueeze(2).to_broadcast([P, BLOCKS, 3]), ALU.mult)
+
+        interleave(nc.scalar, w_bf[1][:], w_raw[1][:])
+        gather_scales(2)
+        us = [product(0, b, True) for b in range(BLOCKS)]
+        gather_words(1, 1)
+        quantize_weight(1)
+        for b in range(BLOCKS):
+            turn(0, b, us[b])
+        interleave(nc.vector, w_bf[2][:], w_raw[2][:])
+        us = [product(1, b, b < 3) for b in range(BLOCKS)]
+        quantize_weight(2)
+        for b in range(BLOCKS):
+            turn(1, b, us[b])
+        gather_words(2, 2)
+
+        out_codes = keep.tile([P, S], U32, name="out_codes", align_bytes=64)
+        out_scales = keep.tile([P, S], U8, name="out_scales", align_bytes=64)
+        out_rows = out_0.rearrange("(p t) j -> p t j", t=PACK)
+        code_rows = out_1[0].rearrange("p c r -> p (c r)").bitcast(I32)
+        us = [product(2, b, b % 2 == 0) for b in range(BLOCKS)]
+        for b in range(BLOCKS):
+            cols = slice(b * P, (b + 1) * P)
+            turn(2, b, us[b])
+            y32 = stage.tile([P, PACK, P], F32, name="y32", align_bytes=64)
+            nc.scalar.copy(y32[:], out_banks[b][:])
+            nc.sync.dma_start(out=out_rows[:, :, cols], in_=y32[:])
+            y16 = stage.tile([P, P, PACK], BF16, name="y16", align_bytes=64)
+            interleave(nc.vector, y16[:], y32[:])
+            nc.vector.quantize_mx(
+                out=out_codes[:, cols].bitcast(FP8X4),
+                scales=out_scales[:, cols],
+                in_=y16[:].rearrange("p j t -> p (j t)"),
+            )
+            if b % 2 == 1:
+                pair = slice((b - 1) * P, (b + 1) * P)
+                nc.sync.dma_start(out=code_rows[:, pair], in_=out_codes[:, pair].bitcast(I32))
+        for q in range(4):
+            eng = nc.sync if q % 2 == 0 else nc.scalar
+            eng.dma_start(
+                out=out_2[0, 4 * q : 4 * q + 4, :].bitcast(I32),
+                in_=out_scales[32 * q : 32 * q + 4, :].bitcast(I32),
+            )

@@ -44,21 +44,20 @@ def tile_picked_yeges_avg_po_kernel(
         word_tab = [keep.tile([P, widths[i]], U32, name=f"word_tab{i}", align_bytes=64) for i in range(3)]
         scale_tab = [keep.tile([P, widths[i]], U8, name=f"scale_tab{i}", align_bytes=64) for i in range(3)]
         att_tab = keep.tile([P, widths[0]], F32, name="att_tab", align_bytes=64)
-        w_raw = [keep.tile([P, PACK, N], F32, name=f"w_raw{i}", align_bytes=64) for i in range(3)]
+        w_raw = [keep.tile([P, PACK, N], F32, name=f"w_raw{i}", align_bytes=64) for i in range(2)]
+        w_raw_half = [keep.tile([P, PACK, N // 2], F32, name=f"w_raw_half{h}", align_bytes=64) for h in range(2)]
         ident = keep.tile([P, P], F32, name="ident", align_bytes=64)
 
-        nc.vector.memset(scale_tab[0][:].bitcast(I32), 0)
-        nc.vector.memset(scale_tab[1][:].bitcast(I32), 0)
         nc.vector.memset(att_tab[:], 0.0)
-        nc.vector.memset(scale_tab[2][:].bitcast(I32), 0)
+        for i in range(3):
+            nc.gpsimd.memset(scale_tab[i][:].bitcast(I32), 0)
         make_identity(nc, ident[:])
 
-        def load_scales(eng, i):
-            for q in range(4):
-                eng.dma_start(
-                    out=scale_tab[i][32 * q : 32 * q + 4, :].bitcast(I32),
-                    in_=scales_in[i][0, 4 * q : 4 * q + 4, :].bitcast(I32),
-                )
+        def load_scale_rows(eng, i, q):
+            eng.dma_start(
+                out=scale_tab[i][32 * q : 32 * q + 4, :].bitcast(I32),
+                in_=scales_in[i][0, 4 * q : 4 * q + 4, :].bitcast(I32),
+            )
 
         def load_words(i):
             nc.sync.dma_start(
@@ -69,37 +68,55 @@ def tile_picked_yeges_avg_po_kernel(
         def load_weight(i):
             nc.sync.dma_start(out=w_raw[i][:], in_=ws[i].rearrange("(p r) n -> p r n", r=PACK))
 
-        for i in range(3):
-            nc.sync.dma_start(lists[i][:], lists_in[i])
-        load_scales(nc.sync, 0)
-        load_weight(0)
-        load_scales(nc.sync, 1)
-        load_words(0)
-        load_weight(1)
-        load_words(1)
-        load_weight(2)
-        load_words(2)
-        for i in range(3):
-            nc.gpsimd.dma_start(out=att_tab[i : i + 1, :], in_=atts[i][0:1, :])
-        load_scales(nc.gpsimd, 2)
+        def load_weight_half(h):
+            nc.sync.dma_start(
+                out=w_raw_half[h][:],
+                in_=ws[2].rearrange("(p r) n -> p r n", r=PACK)[:, :, h * (N // 2) : (h + 1) * (N // 2)],
+            )
 
-        g_words = [keep.tile([P, S], U32, name=f"g_words{i}", align_bytes=64) for i in range(3)]
-        g_scales = [keep.tile([P, S], U8, name=f"g_scales{i}", align_bytes=64) for i in range(3)]
+        def load_att(eng, i):
+            eng.dma_start(out=att_tab[i : i + 1, :], in_=atts[i][0:1, :])
+
+        nc.sync.dma_start(lists[0][:], lists_in[0])
+        nc.sync.dma_start(lists[1][:], lists_in[1])
+        for q in range(3):
+            load_scale_rows(nc.scalar, 0, q)
+        load_scale_rows(nc.sync, 0, 3)
+        load_scale_rows(nc.sync, 1, 0)
+        load_weight(0)
+        for q in range(1, 4):
+            load_scale_rows(nc.sync, 1, q)
+        for i in range(3):
+            load_att(nc.sync, i)
+        load_weight(1)
+        load_words(0)
+        nc.sync.dma_start(lists[2][:], lists_in[2])
+        for q in range(4):
+            load_scale_rows(nc.sync, 2, q)
+        load_words(1)
+        load_weight_half(0)
+        load_weight_half(1)
+        load_words(2)
+
+        g_words, g_scales, w_codes, w_scales = {}, {}, {}, {}
+        g_word_tags = [["g_words0"], ["g_words1"], ["g_words2a", "g_words2b"]]
+        g_scale_tags = ["g_scales0", "g_scales1", "w_raw_half1"]
+        w_code_tags = ["w_codes0", "word_tab1", "w_codes2"]
+        w_scale_tags = ["att_tab", "w_scales1", "w_scales2"]
         w_bf = [keep.tile([P, N, PACK], BF16, name=f"w_bf{i}", align_bytes=64) for i in range(3)]
-        w_codes = [keep.tile([P, N], U32, name=f"w_codes{i}", align_bytes=64) for i in range(3)]
-        w_scales = [keep.tile([P, N], U8, name=f"w_scales{i}", align_bytes=64) for i in range(3)]
         out_banks = [ps_out.tile([P, PACK, P], F32, name=f"out_bank{b}") for b in range(BLOCKS)]
 
         def gather_scales(i):
+            g_scales[i] = keep.tile([P, S], U8, name=g_scale_tags[i], align_bytes=64)
             nc.vector.tensor_copy(g_scales[i][:], scale_tab[i][:].indirect(lists[i][:]))
 
         def gather_words(i, pieces):
             n = S // pieces
             for h in range(pieces):
-                nc.vector.tensor_copy(
-                    g_words[i][:, h * n : (h + 1) * n],
-                    word_tab[i][:].indirect(lists[i][:, h * n // 16 : (h + 1) * n // 16]),
-                )
+                piece = keep.tile([P, n], U32, name=g_word_tags[i][h], align_bytes=64)
+                nc.vector.tensor_copy(piece[:], word_tab[i][:].indirect(lists[i][:, h * n // 16 : (h + 1) * n // 16]))
+                for c in range(n // P):
+                    g_words[i, h * n // P + c] = piece[:, c * P : (c + 1) * P]
 
         def interleave(eng, dst, src):
             d = dst.rearrange("p (c i) r -> p c r i", i=4)
@@ -110,41 +127,44 @@ def tile_picked_yeges_avg_po_kernel(
                 nc.vector.tensor_copy(d, s)
 
         def quantize_weight(i):
+            w_codes[i] = keep.tile([P, N], U32, name=w_code_tags[i], align_bytes=64)
+            w_scales[i] = keep.tile([P, N], U8, name=w_scale_tags[i], align_bytes=64)
             nc.vector.quantize_mx(
                 out=w_codes[i][:].bitcast(FP8X4),
                 scales=w_scales[i][:],
                 in_=w_bf[i][:].rearrange("p n r -> p (n r)"),
             )
 
-        def product(i, b, on_scalar):
+        def product(i, b):
             cols = slice(b * P, (b + 1) * P)
             y = ps_y.tile([P, N], F32, name="y")
             nc.tensor.matmul_mx(
                 out=y[:],
-                lhsT=g_words[i][:, cols].bitcast(FP8X4),
+                lhsT=g_words[i, b].bitcast(FP8X4),
                 lhsT_scale=g_scales[i][:, cols],
                 rhs=w_codes[i][:].bitcast(FP8X4),
                 rhs_scale=w_scales[i][:],
                 start=True,
                 stop=True,
             )
-            u = stage.tile([P, PACK, P], F32, name="u", align_bytes=64)
-            dealt = y[:].rearrange("j (p t) -> j t p", t=PACK)
-            if on_scalar:
-                nc.scalar.activation(u[:], dealt, ACT.Copy, scale=share[:, b, i : i + 1])
-            else:
-                nc.vector.tensor_scalar(u[:], dealt, share[:, b, i : i + 1], None, ALU.mult)
-            return u
+            return y[:].rearrange("j (p t) -> j t p", t=PACK)
 
-        def turn(i, b, u):
+        def weighted(i, b, u):
+            nc.scalar.activation(u, product(i, b), ACT.Copy, scale=share[:, b, i : i + 1])
+
+        def weighted_onto(i, b, u):
+            dealt = product(i, b)
+            nc.vector.scalar_tensor_tensor(u, dealt, share[:, b, i : i + 1], u, ALU.mult, ALU.add)
+
+        def turn(b, u, first=False, last=False):
             for t in range(PACK):
                 nc.tensor.matmul(
                     out_banks[b][:, t, :],
                     lhsT=u[:, t, :],
                     rhs=ident[:],
                     is_transpose=True,
-                    start=(i == 0 and t == 0),
-                    stop=(i == 2 and t == PACK - 1),
+                    start=(first and t == 0),
+                    stop=(last and t == PACK - 1),
                 )
 
         gather_scales(0)
@@ -156,43 +176,50 @@ def tile_picked_yeges_avg_po_kernel(
         att_t = ps_y.tile([P, BLOCKS, P], F32, name="y")
         for b in range(BLOCKS):
             nc.tensor.transpose(att_t[:, b, :], g_att[:, b * P : (b + 1) * P], ident[:])
-        top = keep.tile([P, BLOCKS], F32, name="top")
-        shifted = keep.tile([P, BLOCKS, 3], F32, name="shifted")
-        expd = keep.tile([P, BLOCKS, 3], F32, name="w_raw0", align_bytes=64)
+        quantize_weight(0)
+        neg_top = keep.tile([P, BLOCKS], F32, name="neg_top")
+        nc.vector.tensor_reduce(neg_top[:], att_t[:, :, 0:3], AX.X, ALU.max, negate=True)
+        interleave(nc.scalar, w_bf[1][:], w_raw[1][:])
+        gather_words(0, 1)
+        expd = keep.tile([P, BLOCKS, 3], F32, name="w_raw1", align_bytes=64)
         den = keep.tile([P, BLOCKS], F32, name="den")
         rden = keep.tile([P, BLOCKS], F32, name="rden")
         share = keep.tile([P, BLOCKS, 3], F32, name="share")
-        gather_words(0, 1)
-        nc.vector.tensor_reduce(top[:], att_t[:, :, 0:3], AX.X, ALU.max)
-        nc.vector.tensor_tensor(shifted[:], att_t[:, :, 0:3], top[:].unsqueeze(2).to_broadcast([P, BLOCKS, 3]), ALU.subtract)
-        nc.scalar.activation(expd[:], shifted[:], ACT.Exp)
-        quantize_weight(0)
-        nc.vector.tensor_reduce(den[:], expd[:], AX.X, ALU.add)
+        for b in range(BLOCKS):
+            nc.scalar.activation(
+                expd[:, b, :], att_t[:, b, 0:3], ACT.Exp, bias=neg_top[:, b : b + 1], accum_out=den[:, b : b + 1]
+            )
         nc.vector.reciprocal(rden[:], den[:])
         nc.vector.tensor_tensor(share[:], expd[:], rden[:].unsqueeze(2).to_broadcast([P, BLOCKS, 3]), ALU.mult)
-
-        interleave(nc.scalar, w_bf[1][:], w_raw[1][:])
-        gather_scales(2)
-        us = [product(0, b, True) for b in range(BLOCKS)]
+        u0 = keep.tile([P, BLOCKS, PACK, P], F32, name="u0", align_bytes=64)
+        for b in range(BLOCKS):
+            weighted(0, b, u0[:, b])
         gather_words(1, 1)
         quantize_weight(1)
         for b in range(BLOCKS):
-            turn(0, b, us[b])
-        interleave(nc.vector, w_bf[2][:], w_raw[2][:])
-        us = [product(1, b, b < 3) for b in range(BLOCKS)]
+            turn(b, u0[:, b], first=True)
+        interleave(nc.scalar, w_bf[2][:, : N // 2, :], w_raw_half[0][:])
+        interleave(nc.vector, w_bf[2][:, N // 2 :, :], w_raw_half[1][:])
+        gather_scales(2)
         quantize_weight(2)
-        for b in range(BLOCKS):
-            turn(1, b, us[b])
+        u1 = keep.tile([P, BLOCKS, PACK, P], F32, name="w_raw_half0", align_bytes=64)
+        last_block = BLOCKS - 1
+        for b in [last_block] + list(range(last_block)):
+            weighted(1, b, u1[:, b])
+        turn(last_block, u1[:, last_block])
         gather_words(2, 2)
 
         out_codes = keep.tile([P, S], U32, name="out_codes", align_bytes=64)
         out_scales = keep.tile([P, S], U8, name="out_scales", align_bytes=64)
         out_rows = out_0.rearrange("(p t) j -> p t j", t=PACK)
         code_rows = out_1[0].rearrange("p c r -> p (c r)").bitcast(I32)
-        us = [product(2, b, b % 2 == 0) for b in range(BLOCKS)]
+        u2 = keep.tile([P, PACK, P], F32, name="u2", align_bytes=64)
+        for b in range(last_block):
+            weighted_onto(2, b, u1[:, b])
+        weighted(2, last_block, u2[:])
         for b in range(BLOCKS):
             cols = slice(b * P, (b + 1) * P)
-            turn(2, b, us[b])
+            turn(b, u2[:] if b == last_block else u1[:, b], last=True)
             y32 = stage.tile([P, PACK, P], F32, name="y32", align_bytes=64)
             nc.scalar.copy(y32[:], out_banks[b][:])
             nc.sync.dma_start(out=out_rows[:, :, cols], in_=y32[:])

@@ -55,7 +55,7 @@ def tile_picked_yeges_avg_po_kernel(
 
         def load_scale_rows(eng, i, q):
             eng.dma_start(
-                out=scale_tab[i][32 * q : 32 * q + 4, :].bitcast(I32),
+                out=scale_tab[i][32 * q + 4 * i : 32 * q + 4 * i + 4, :].bitcast(I32),
                 in_=scales_in[i][0, 4 * q : 4 * q + 4, :].bitcast(I32),
             )
 
@@ -75,7 +75,7 @@ def tile_picked_yeges_avg_po_kernel(
             )
 
         def load_att(eng, i):
-            eng.dma_start(out=att_tab[i : i + 1, :], in_=atts[i][0:1, :])
+            eng.dma_start(out=att_tab[12 + 4 * i : 13 + 4 * i, :], in_=atts[i][0:1, :])
 
         nc.sync.dma_start(lists[0][:], lists_in[0])
         nc.sync.dma_start(lists[1][:], lists_in[1])
@@ -126,6 +126,14 @@ def tile_picked_yeges_avg_po_kernel(
             else:
                 nc.vector.tensor_copy(d, s)
 
+        def deal(eng, i, src, first, count):
+            d = w_bf[i][:].rearrange("p (t m) r -> p m r t", t=PACK)[:, first : first + count]
+            s = src.rearrange("p r (m t) -> p m r t", t=PACK)
+            if eng is nc.scalar:
+                nc.scalar.copy(d, s)
+            else:
+                nc.vector.tensor_copy(d, s)
+
         def quantize_weight(i):
             w_codes[i] = keep.tile([P, N], U32, name=w_code_tags[i], align_bytes=64)
             w_scales[i] = keep.tile([P, N], U8, name=w_scale_tags[i], align_bytes=64)
@@ -141,13 +149,13 @@ def tile_picked_yeges_avg_po_kernel(
             nc.tensor.matmul_mx(
                 out=y[:],
                 lhsT=g_words[i, b].bitcast(FP8X4),
-                lhsT_scale=g_scales[i][:, cols],
+                lhsT_scale=g_scales[i][4 * i :, cols],
                 rhs=w_codes[i][:].bitcast(FP8X4),
                 rhs_scale=w_scales[i][:],
                 start=True,
                 stop=True,
             )
-            return y[:].rearrange("j (p t) -> j t p", t=PACK)
+            return y[:].rearrange("j (t p) -> j t p", t=PACK)
 
         def weighted(i, b, u):
             nc.scalar.activation(u, product(i, b), ACT.Copy, scale=share[:, b, i : i + 1])
@@ -168,7 +176,7 @@ def tile_picked_yeges_avg_po_kernel(
                 )
 
         gather_scales(0)
-        interleave(nc.scalar, w_bf[0][:], w_raw[0][:])
+        deal(nc.scalar, 0, w_raw[0][:], 0, P)
         gather_scales(1)
 
         g_att = keep.tile([P, S], F32, name="g_att", align_bytes=64)
@@ -178,8 +186,8 @@ def tile_picked_yeges_avg_po_kernel(
             nc.tensor.transpose(att_t[:, b, :], g_att[:, b * P : (b + 1) * P], ident[:])
         quantize_weight(0)
         neg_top = keep.tile([P, BLOCKS], F32, name="neg_top")
-        nc.vector.tensor_reduce(neg_top[:], att_t[:, :, 0:3], AX.X, ALU.max, negate=True)
-        interleave(nc.scalar, w_bf[1][:], w_raw[1][:])
+        nc.vector.tensor_reduce(neg_top[:], att_t[:, :, 12:24:4], AX.X, ALU.max, negate=True)
+        deal(nc.scalar, 1, w_raw[1][:], 0, P)
         gather_words(0, 1)
         expd = keep.tile([P, BLOCKS, 3], F32, name="w_raw1", align_bytes=64)
         den = keep.tile([P, BLOCKS], F32, name="den")
@@ -187,7 +195,7 @@ def tile_picked_yeges_avg_po_kernel(
         share = keep.tile([P, BLOCKS, 3], F32, name="share")
         for b in range(BLOCKS):
             nc.scalar.activation(
-                expd[:, b, :], att_t[:, b, 0:3], ACT.Exp, bias=neg_top[:, b : b + 1], accum_out=den[:, b : b + 1]
+                expd[:, b, :], att_t[:, b, 12:24:4], ACT.Exp, bias=neg_top[:, b : b + 1], accum_out=den[:, b : b + 1]
             )
         nc.vector.reciprocal(rden[:], den[:])
         nc.vector.tensor_tensor(share[:], expd[:], rden[:].unsqueeze(2).to_broadcast([P, BLOCKS, 3]), ALU.mult)
@@ -198,28 +206,24 @@ def tile_picked_yeges_avg_po_kernel(
         quantize_weight(1)
         for b in range(BLOCKS):
             turn(b, u0[:, b], first=True)
-        interleave(nc.scalar, w_bf[2][:, : N // 2, :], w_raw_half[0][:])
-        interleave(nc.vector, w_bf[2][:, N // 2 :, :], w_raw_half[1][:])
+        deal(nc.scalar, 2, w_raw_half[0][:], 0, P // 2)
+        deal(nc.vector, 2, w_raw_half[1][:], P // 2, P // 2)
         gather_scales(2)
         quantize_weight(2)
         u1 = keep.tile([P, BLOCKS, PACK, P], F32, name="w_raw_half0", align_bytes=64)
-        last_block = BLOCKS - 1
-        for b in [last_block] + list(range(last_block)):
+        for b in range(BLOCKS):
             weighted(1, b, u1[:, b])
-        turn(last_block, u1[:, last_block])
         gather_words(2, 2)
 
         out_codes = keep.tile([P, S], U32, name="out_codes", align_bytes=64)
         out_scales = keep.tile([P, S], U8, name="out_scales", align_bytes=64)
         out_rows = out_0.rearrange("(p t) j -> p t j", t=PACK)
         code_rows = out_1[0].rearrange("p c r -> p (c r)").bitcast(I32)
-        u2 = keep.tile([P, PACK, P], F32, name="u2", align_bytes=64)
-        for b in range(last_block):
+        for b in range(BLOCKS):
             weighted_onto(2, b, u1[:, b])
-        weighted(2, last_block, u2[:])
         for b in range(BLOCKS):
             cols = slice(b * P, (b + 1) * P)
-            turn(b, u2[:] if b == last_block else u1[:, b], last=True)
+            turn(b, u1[:, b], last=True)
             y32 = stage.tile([P, PACK, P], F32, name="y32", align_bytes=64)
             nc.scalar.copy(y32[:], out_banks[b][:])
             nc.sync.dma_start(out=out_rows[:, :, cols], in_=y32[:])

from contextlib import ExitStack

import concourse.mybir as mybir
from concourse.masks import make_identity

F32 = mybir.dt.float32
BF16 = mybir.dt.bfloat16
I32 = mybir.dt.int32
U32 = mybir.dt.uint32
U16 = mybir.dt.uint16
U8 = mybir.dt.uint8
FP8X4 = mybir.dt.float8_e4m3fn_x4
ALU = mybir.AluOpType
ACT = mybir.ActivationFunctionType
AX = mybir.AxisListType

P = 128
PACK = 4
S = 512
N = 512
K = 512
BLOCKS = S // P
FLOPS = 3 * 2 * K * N * S


def tile_picked_yeges_avg_po_kernel(
    tc, x_words, x_scales, e_words, e_scales, d_words, d_scales, att0, att1, att2, w1, w2, w3, offs, shop, brand, out_0, out_1, out_2
):
    nc = tc.nc
    words_in = [x_words, e_words, d_words]
    scales_in = [x_scales, e_scales, d_scales]
    lists_in = [offs, shop, brand]
    atts = [att0, att1, att2]
    ws = [w1, w2, w3]
    widths = [w.shape[2] for w in words_in]

    with ExitStack() as ctx:
        keep = ctx.enter_context(tc.tile_pool(name="keep", bufs=1))
        stage = ctx.enter_context(tc.tile_pool(name="stage", bufs=4))
        ps_out = ctx.enter_context(tc.psum_pool(name="ps_out", bufs=1))
        ps_y = ctx.enter_context(tc.psum_pool(name="ps_y", bufs=4))

        lists = [keep.tile([P, S // 16], U16, name=f"list{i}") for i in range(3)]
        word_tab = [keep.tile([P, widths[i]], U32, name=f"word_tab{i}", align_bytes=64) for i in range(3)]
        scale_tab = [keep.tile([P, widths[i]], U8, name=f"scale_tab{i}", align_bytes=64) for i in range(3)]
        att_tab = keep.tile([P, widths[0]], F32, name="att_tab", align_bytes=64)
        w_raw = [keep.tile([P, PACK, N], F32, name=f"w_raw{i}", align_bytes=64) for i in range(2)]
        w_raw_half = [keep.tile([P, PACK, N // 2], F32, name=f"w_raw_half{h}", align_bytes=64) for h in range(2)]
        ident = keep.tile([P, P], F32, name="ident", align_bytes=64)

        nc.vector.memset(att_tab[:], 0.0)
        for i in range(3):
            nc.gpsimd.memset(scale_tab[i][:].bitcast(I32), 0)
        make_identity(nc, ident[:])

        def load_scale_rows(eng, i, q):
            eng.dma_start(
                out=scale_tab[i][32 * q + 4 * i : 32 * q + 4 * i + 4, :].bitcast(I32),
                in_=scales_in[i][0, 4 * q : 4 * q + 4, :].bitcast(I32),
            )

        def load_words(i):
            nc.sync.dma_start(
                out=word_tab[i][:].bitcast(I32),
                in_=words_in[i][0].rearrange("p c r -> p (c r)").bitcast(I32),
            )

        def load_weight(i):
            nc.sync.dma_start(out=w_raw[i][:], in_=ws[i].rearrange("(p r) n -> p r n", r=PACK))

        def load_weight_half(h):
            nc.sync.dma_start(
                out=w_raw_half[h][:],
                in_=ws[2].rearrange("(p r) n -> p r n", r=PACK)[:, :, h * (N // 2) : (h + 1) * (N // 2)],
            )

        def load_att(eng, i):
            eng.dma_start(out=att_tab[12 + 4 * i : 13 + 4 * i, :], in_=atts[i][0:1, :])

        nc.sync.dma_start(lists[0][:], lists_in[0])
        nc.sync.dma_start(lists[1][:], lists_in[1])
        for q in range(3):
            load_scale_rows(nc.scalar, 0, q)
        load_scale_rows(nc.sync, 0, 3)
        load_scale_rows(nc.sync, 1, 0)
        load_weight(0)
        for q in range(1, 4):
            load_scale_rows(nc.sync, 1, q)
        for i in range(3):
            load_att(nc.sync, i)
        load_weight(1)
        load_words(0)
        nc.sync.dma_start(lists[2][:], lists_in[2])
        for q in range(4):
            load_scale_rows(nc.sync, 2, q)
        load_words(1)
        load_weight_half(0)
        load_weight_half(1)
        load_words(2)

        g_words, g_scales, w_codes, w_scales = {}, {}, {}, {}
        g_word_tags = [["g_words0"], ["g_words1"], ["g_words2a", "g_words2b"]]
        g_scale_tags = ["g_scales0", "g_scales1", "w_raw_half1"]
        w_code_tags = ["w_codes0", "word_tab1", "w_codes2"]
        w_scale_tags = ["att_tab", "w_scales1", "w_scales2"]
        w_bf = [keep.tile([P, N, PACK], BF16, name=f"w_bf{i}", align_bytes=64) for i in range(3)]
        out_banks = [ps_out.tile([P, PACK, P], F32, name=f"out_bank{b}") for b in range(BLOCKS)]

        def gather_scales(i):
            g_scales[i] = keep.tile([P, S], U8, name=g_scale_tags[i], align_bytes=64)
            nc.vector.tensor_copy(g_scales[i][:], scale_tab[i][:].indirect(lists[i][:]))

        def gather_words(i, pieces):
            n = S // pieces
            for h in range(pieces):
                piece = keep.tile([P, n], U32, name=g_word_tags[i][h], align_bytes=64)
                nc.vector.tensor_copy(piece[:], word_tab[i][:].indirect(lists[i][:, h * n // 16 : (h + 1) * n // 16]))
                for c in range(n // P):
                    g_words[i, h * n // P + c] = piece[:, c * P : (c + 1) * P]

        def interleave(eng, dst, src):
            d = dst.rearrange("p (c i) r -> p c r i", i=4)
            s = src.rearrange("p r (c i) -> p c r i", i=4)
            if eng is nc.scalar:
                nc.scalar.copy(d, s)
            else:
                nc.vector.tensor_copy(d, s)

        def deal(eng, i, src, first, count):
            d = w_bf[i][:].rearrange("p (t m) r -> p m r t", t=PACK)[:, first : first + count]
            s = src.rearrange("p r (m t) -> p m r t", t=PACK)
            if eng is nc.scalar:
                nc.scalar.copy(d, s)
            else:
                nc.vector.tensor_copy(d, s)

        def quantize_weight(i):
            w_codes[i] = keep.tile([P, N], U32, name=w_code_tags[i], align_bytes=64)
            w_scales[i] = keep.tile([P, N], U8, name=w_scale_tags[i], align_bytes=64)
            nc.vector.quantize_mx(
                out=w_codes[i][:].bitcast(FP8X4),
                scales=w_scales[i][:],
                in_=w_bf[i][:].rearrange("p n r -> p (n r)"),
            )

        def product(i, b):
            cols = slice(b * P, (b + 1) * P)
            y = ps_y.tile([P, N], F32, name="y")
            nc.tensor.matmul_mx(
                out=y[:],
                lhsT=g_words[i, b].bitcast(FP8X4),
                lhsT_scale=g_scales[i][4 * i :, cols],
                rhs=w_codes[i][:].bitcast(FP8X4),
                rhs_scale=w_scales[i][:],
                start=True,
                stop=True,
            )
            return y[:].rearrange("j (t p) -> j t p", t=PACK)

        def weighted(i, b, u):
            nc.scalar.activation(u, product(i, b), ACT.Copy, scale=share[:, b, i : i + 1])

        def weighted_onto(i, b, u):
            dealt = product(i, b)
            nc.vector.scalar_tensor_tensor(u, dealt, share[:, b, i : i + 1], u, ALU.mult, ALU.add)

        def turn(b, u, first=False, last=False):
            for t in range(PACK):
                nc.tensor.matmul(
                    out_banks[b][:, t, :],
                    lhsT=u[:, t, :],
                    rhs=ident[:],
                    is_transpose=True,
                    start=(first and t == 0),
                    stop=(last and t == PACK - 1),
                )

        gather_scales(0)
        deal(nc.scalar, 0, w_raw[0][:], 0, P)
        gather_scales(1)

        g_att = keep.tile([P, S], F32, name="g_att", align_bytes=64)
        nc.vector.tensor_copy(g_att[:], att_tab[:].indirect(lists[0][:]))
        att_t = ps_y.tile([P, BLOCKS, P], F32, name="y")
        for b in range(BLOCKS):
            nc.tensor.transpose(att_t[:, b, :], g_att[:, b * P : (b + 1) * P], ident[:])
        quantize_weight(0)
        neg_top = keep.tile([P, BLOCKS], F32, name="neg_top")
        nc.vector.tensor_reduce(neg_top[:], att_t[:, :, 12:24:4], AX.X, ALU.max, negate=True)
        deal(nc.scalar, 1, w_raw[1][:], 0, P)
        gather_words(0, 1)
        expd = keep.tile([P, BLOCKS, 3], F32, name="w_raw1", align_bytes=64)
        den = keep.tile([P, BLOCKS], F32, name="den")
        rden = keep.tile([P, BLOCKS], F32, name="rden")
        share = keep.tile([P, BLOCKS, 3], F32, name="share")
        for b in range(BLOCKS):
            nc.scalar.activation(
                expd[:, b, :], att_t[:, b, 12:24:4], ACT.Exp, bias=neg_top[:, b : b + 1], accum_out=den[:, b : b + 1]
            )
        nc.vector.reciprocal(rden[:], den[:])
        nc.vector.tensor_tensor(share[:], expd[:], rden[:].unsqueeze(2).to_broadcast([P, BLOCKS, 3]), ALU.mult)
        u0 = keep.tile([P, BLOCKS, PACK, P], F32, name="u0", align_bytes=64)
        for b in range(BLOCKS):
            weighted(0, b, u0[:, b])
        gather_words(1, 1)
        quantize_weight(1)
        for b in range(BLOCKS):
            turn(b, u0[:, b], first=True)
        deal(nc.scalar, 2, w_raw_half[0][:], 0, P // 2)
        deal(nc.vector, 2, w_raw_half[1][:], P // 2, P // 2)
        gather_scales(2)
        quantize_weight(2)
        u1 = keep.tile([P, BLOCKS, PACK, P], F32, name="w_raw_half0", align_bytes=64)
        for b in range(BLOCKS):
            weighted(1, b, u1[:, b])
        gather_words(2, 2)

        out_codes = keep.tile([P, S], U32, name="out_codes", align_bytes=64)
        out_scales = keep.tile([P, S], U8, name="out_scales", align_bytes=64)
        out_rows = out_0.rearrange("(p t) j -> p t j", t=PACK)
        code_rows = out_1[0].rearrange("p c r -> p (c r)").bitcast(I32)
        for b in range(BLOCKS):
            weighted_onto(2, b, u1[:, b])
        for b in range(BLOCKS):
            cols = slice(b * P, (b + 1) * P)
            turn(b, u1[:, b], last=True)
            y32 = stage.tile([P, PACK, P], F32, name="y32", align_bytes=64)
            nc.scalar.copy(y32[:], out_banks[b][:])
            nc.sync.dma_start(out=out_rows[:, :, cols], in_=y32[:])
            y16 = stage.tile([P, P, PACK], BF16, name="y16", align_bytes=64)
            interleave(nc.vector, y16[:], y32[:])
            nc.vector.quantize_mx(
                out=out_codes[:, cols].bitcast(FP8X4),
                scales=out_scales[:, cols],
                in_=y16[:].rearrange("p j t -> p (j t)"),
            )
            if b % 2 == 1:
                pair = slice((b - 1) * P, (b + 1) * P)
                nc.sync.dma_start(out=code_rows[:, pair], in_=out_codes[:, pair].bitcast(I32))
        for q in range(4):
            eng = nc.sync if q % 2 == 0 else nc.scalar
            eng.dma_start(
                out=out_2[0, 4 * q : 4 * q + 4, :].bitcast(I32),
                in_=out_scales[32 * q : 32 * q + 4, :].bitcast(I32),
            )
